import numpy as np
import ml_dtypes


def mxq(x, axis, fmt="e4m3"):
    dtype, down = {"e4m3": (ml_dtypes.float8_e4m3fn, 7), "e5m2": (ml_dtypes.float8_e5m2, 14)}[fmt]
    v = np.moveaxis(np.asarray(x, np.float32).astype(ml_dtypes.bfloat16).astype(np.float64), axis, -1)
    blocks = v.reshape(v.shape[:-1] + (-1, 32))
    amax = np.abs(blocks).max(-1, keepdims=True)
    byte = np.maximum(np.where(amax > 0, np.frexp(amax)[1] - 1 + 127, 0) - down, 1)
    scale = np.exp2(byte - 127.0)
    codes = (blocks / scale).astype(np.float32).astype(dtype).astype(np.float64)
    return np.moveaxis((codes * scale).reshape(v.shape), -1, axis)


WIDE = False


def mx_kscale(k):
    if not WIDE:
        return np.ones(k)
    levels = np.array([10, -10, 5, -5, 0])
    if k % 512:
        return np.exp2(np.random.permutation(np.resize(levels, k // 32))).repeat(32)
    a = np.empty((k // 512, 16))
    for p in range(k // 512):
        a[p, :8] = np.random.permutation(np.resize(levels, 8))
        for g in range(8):
            far = levels[np.abs(levels - a[p, g]) >= 10]
            a[p, g + 8] = far[np.random.randint(len(far))]
    return np.exp2(a.ravel()).repeat(32)


def f64(x):
    return np.asarray(x).astype(np.float64)


def striped(idx):
    return np.tile(idx.reshape(-1, 16).T, (8, 1)).astype(np.uint16)


def unstriped(offs):
    return offs[:16].T.reshape(-1).astype(np.int64)


E2M1 = np.array([0.0, 0.5, 1.0, 1.5, 2.0, 3.0, 4.0, 6.0, -0.0, -0.5, -1.0, -1.5, -2.0, -3.0, -4.0, -6.0])


def pack_weight(w, fmt):
    k, n = w.shape
    w = f64(np.asarray(w, np.float32).astype(ml_dtypes.bfloat16)).reshape(k // 32, 32, n)
    amax = np.abs(w).max(1)
    if fmt == "e4m3":
        byte = np.frexp(amax)[1] - 1 + 127 - 7
    else:
        mant, ex = np.frexp(amax / 6.0)
        byte = np.where(mant > 0.5, ex, ex - 1) + 127
    byte = np.clip(np.where(amax > 0, byte, 1), 1, 254)
    scaled = (w * np.exp2(127.0 - byte)[:, None, :]).reshape(k, n).astype(np.float32)
    by_word = np.ascontiguousarray(scaled.reshape(k // 512, 128, 4, n).transpose(0, 1, 3, 2))
    if fmt == "e4m3":
        words = by_word.astype(ml_dtypes.float8_e4m3fn).view(np.uint8)
    else:
        c = by_word.astype(ml_dtypes.float4_e2m1fn).view(np.uint8) & 0xF
        words = (c[..., 0::2] | (c[..., 1::2] << 4)).reshape(k // 512, 128, 2 * n)
    return np.ascontiguousarray(words), np.ascontiguousarray(byte.astype(np.uint8).reshape(k // 512, 16, n))


def unpack_weight(words, scales, fmt):
    g, _, n = scales.shape
    words = np.ascontiguousarray(words).reshape(g, 128, n, -1)
    if fmt == "e4m3":
        vals = words.view(ml_dtypes.float8_e4m3fn).astype(np.float64)
    else:
        nib = np.empty((g, 128, n, 4), np.uint8)
        nib[..., 0::2] = words & 0xF
        nib[..., 1::2] = words >> 4
        vals = E2M1[nib]
    vals = vals * np.repeat(np.exp2(scales.astype(np.float64) - 127.0), 8, axis=1)[..., None]
    return vals.transpose(0, 1, 3, 2).reshape(g * 512, n)


def relu(v):
    return np.maximum(v, 0.0)


K, T, E, C, N = 512, 640, 2, 256, 1024
M = 128


def by_expert(wq, xq):
    return np.concatenate([wq[e].T @ xq[:, e * C:(e + 1) * C] for e in range(E)], axis=1)


def setup_inputs():
    n = np.random.standard_normal
    s = mx_kscale(K)[:, None]
    v = mx_kscale(N)
    w = [pack_weight(m, "e2m1") for m in n((E, K, N)) / np.sqrt(K) / s[None] * v[None, None, :]]
    return {
        "xT": (n((K, T)) * s).astype(np.float32),
        "w_words": np.stack([m[0] for m in w]),
        "w_scales": np.stack([m[1] for m in w]),
        "b": (0.3 * n((N, E)) * v[:, None]).astype(np.float32),
        "wp": (n((N, M)) / np.sqrt(N) / v[:, None]).astype(np.float32),
        "gate": np.tile(np.random.uniform(0.2, 1.0, E * C), (N, 1)).astype(np.float32),
        "offs": striped(np.random.permutation(T)[:E * C]),
    }


def reference(xT, w_words, w_scales, b, wp, gate, offs):
    idx = unstriped(offs)
    w = np.stack([unpack_weight(w_words[e], w_scales[e], "e2m1") for e in range(E)])
    xq = mxq(f64(xT)[:, idx], 0, "e4m3")
    y = by_expert(w, xq)
    y = relu(y + np.repeat(f64(b), C, axis=1))
    c = np.zeros((N, T))
    c[:, idx] = f64(gate) * y
    return mxq(f64(wp), 0, "e4m3").T @ mxq(c, 0, "e4m3")

@@ -1,0 +1,197 @@
+from contextlib import ExitStack
+
+import concourse.mybir as mybir
+
+K, T, E, C, N, M = 512, 640, 2, 256, 1024, 128
+P = 128
+PACK = 4
+PASSES = N // 512
+
+FLOPS = 2 * E * C * K * N + 2 * E * C * N * M
+BYTES = 4 * K * T + E * K * N // 2 + E * K * N // 32 + 4 * N * E + 4 * N * M + 4 * E * C + 2 * P * (E * C // 16) + 4 * M * T
+
+F32 = mybir.dt.float32
+BF16 = mybir.dt.bfloat16
+I32 = mybir.dt.int32
+U32 = mybir.dt.uint32
+U16 = mybir.dt.uint16
+U8 = mybir.dt.uint8
+FP8X4 = mybir.dt.float8_e4m3fn_x4
+FP4X4 = mybir.dt.float4_e2m1fn_x4
+RELU = mybir.ActivationFunctionType.Relu
+ADD = mybir.AluOpType.add
+MULT = mybir.AluOpType.mult
+
+
+def tile_moe_nxt_lin_relu_kernel(tc, xT, w_words, w_scales, b, wp, gate, offs, out):
+    nc = tc.nc
+    with ExitStack() as ctx:
+        keep = ctx.enter_context(tc.tile_pool(name="keep", bufs=1))
+        psum1 = ctx.enter_context(tc.psum_pool(name="psum1", bufs=6))
+        psum2 = ctx.enter_context(tc.psum_pool(name="psum2", bufs=2))
+
+        offsets = keep.tile([P, E * C // 16], U16, name="offsets")
+        w_raw = keep.tile([P, E, 2 * N], U8, align_bytes=64, name="w_raw")
+        w_perm = keep.tile([P, E, 2 * N], U8, align_bytes=64, name="w_perm")
+        s_raw = keep.tile([P, E, N], U8, align_bytes=64, name="s_raw")
+        s_perm = keep.tile([P, E, N], U8, align_bytes=64, name="s_perm")
+        codes = keep.tile([P, T], U32, align_bytes=64, name="codes")
+        scales = keep.tile([P, T], U8, align_bytes=64, name="scales")
+        bias = keep.tile([P, PASSES, PACK, E], F32, name="bias")
+        gates = keep.tile([P, E * C], F32, name="gates")
+        wp_raw = keep.tile([P, PASSES, PACK, M], F32, name="wp_raw")
+        wp_bf = keep.tile([P, PASSES, M, PACK], BF16, align_bytes=64, name="wp_bf")
+        wp_codes = keep.tile([P, PASSES * M], U32, align_bytes=64, name="wp_codes")
+        wp_scales = keep.tile([P, PASSES * M], U8, align_bytes=64, name="wp_scales")
+        result = keep.tile([P, T], F32, name="result")
+
+        nc.vector.memset(s_raw[:].rearrange("p e n -> p (e n)").bitcast(I32), 0)
+        nc.vector.memset(scales[:].bitcast(I32), 0)
+        nc.vector.memset(result[:], 0.0)
+        b_rows = b.rearrange("(a h t i) e -> a i h t e", a=PASSES, t=PACK, i=2)
+        for a in range(PASSES):
+            for i in range(2):
+                nc.gpsimd.dma_start(out=bias[i:P:2, a, :, :], in_=b_rows[a, i])
+        wp_rows = wp.rearrange("(a h t i) f -> a i h t f", a=PASSES, t=PACK, i=2)
+        x_rows = xT.rearrange("(p j) t -> p j t", j=PACK)
+        chunks = [(0, 256, 96), (256, 256, 96), (512, 128, 48)]
+        x_raw = []
+        for t0, width, cut in chunks:
+            x_raw.append(keep.tile([P, PACK, width], F32, name="x_raw%d" % t0))
+
+        def load_words(e):
+            nc.sync.dma_start(out=w_raw[:, e, :].bitcast(I32), in_=w_words[e, 0].bitcast(I32))
+
+        load_words(0)
+        for q in range(4):
+            nc.sync.dma_start(
+                out=s_raw[32 * q : 32 * q + 4, :, :].bitcast(I32),
+                in_=w_scales[:, 0, 4 * q : 4 * q + 4, :].rearrange("e q n -> q e n").bitcast(I32),
+            )
+        for (t0, width, cut), raw in zip(chunks, x_raw):
+            nc.sync.dma_start(out=raw[:], in_=x_rows[:, :, t0 : t0 + width])
+        nc.sync.dma_start(offsets[:], offs)
+        for a in range(PASSES):
+            for i in range(2):
+                nc.sync.dma_start(out=wp_raw[i:P:2, a, :, :], in_=wp_rows[a, i])
+        load_words(1)
+        nc.sync.dma_start(out=gates[:], in_=gate[0:P, :])
+
+        def permute(engine, dst, src, dt):
+            engine.tensor_copy(
+                out=dst.bitcast(dt).rearrange("p (a t h) -> p a t h", a=PASSES, t=PACK),
+                in_=src.bitcast(dt).rearrange("p (a h t) -> p a t h", a=PASSES, t=PACK),
+            )
+
+        permute(nc.vector, w_perm[:, 0, :], w_raw[:, 0, :], I32)
+        for e in range(E):
+            permute(nc.vector, s_perm[:, e, :], s_raw[:, e, :], U16)
+
+        def four(x):
+            return x.rearrange("p (c i) t -> p c t i", i=4)
+
+        def four_in(x):
+            return x.rearrange("p t (c i) -> p c t i", i=4)
+
+        for (t0, width, cut), raw in zip(chunks, x_raw):
+            grouped = keep.tile([P, width, PACK], BF16, align_bytes=64, name="x_bf%d" % t0)
+            nc.scalar.copy(out=four(grouped[:, 0:cut, :]), in_=four_in(raw[:, :, 0:cut]))
+            nc.vector.tensor_copy(out=four(grouped[:, cut:width, :]), in_=four_in(raw[:, :, cut:width]))
+            nc.vector.quantize_mx(
+                out=codes[:, t0 : t0 + width].bitcast(FP8X4),
+                scales=scales[:, t0 : t0 + width],
+                in_=grouped[:].rearrange("p t j -> p (t j)"),
+            )
+
+        for a in range(PASSES):
+            nc.gpsimd.tensor_scalar(
+                out=four(wp_bf[:, a]), in0=four_in(wp_raw[:, a]), scalar1=1.0, scalar2=0.0, op0=MULT, op1=ADD
+            )
+
+        slot_codes = []
+        slot_scales = []
+        for e in range(E):
+            own = offsets[:, e * C // 16 : (e + 1) * C // 16]
+            sc = keep.tile([P, C], U32, align_bytes=64, name="slot_codes%d" % e)
+            ss = keep.tile([P, C], U8, align_bytes=64, name="slot_scales%d" % e)
+            nc.vector.tensor_copy(sc[:], codes[:].indirect(own))
+            nc.vector.tensor_copy(ss[:], scales[:].indirect(own))
+            slot_codes.append(sc)
+            slot_scales.append(ss)
+
+        permute(nc.vector, w_perm[:, 1, :], w_raw[:, 1, :], I32)
+
+        hidden = {}
+        for e in range(E):
+            for a in range(PASSES):
+                h = keep.tile([P, PACK, C], F32, name="hidden%d%d" % (e, a))
+                hidden[e, a] = h
+                for half in range(2):
+                    bank = psum1.tile([P, 2, C], F32, name="bank")
+                    for i in range(2):
+                        t = 2 * half + i
+                        c0 = (a * PACK + t) * P
+                        nc.tensor.matmul_mx(
+                            out=bank[:, i, :],
+                            lhsT=w_perm[:, e, 2 * c0 : 2 * (c0 + P)].bitcast(FP4X4),
+                            lhsT_scale=s_perm[:, e, c0 : c0 + P],
+                            rhs=slot_codes[e][:].bitcast(FP8X4),
+                            rhs_scale=slot_scales[e][:],
+                            start=True,
+                            stop=True,
+                        )
+                        own_bias = bias[:, a, t, e : e + 1]
+                        nc.scalar.activation(out=h[:, t, :], in_=bank[:, i, :], func=RELU, bias=own_bias)
+
+        def gated(e, a):
+            g = keep.tile([P, C, PACK], BF16, align_bytes=64, name="gated%d%d" % (e, a))
+            nc.vector.tensor_tensor(
+                out=four(g[:]),
+                in0=four_in(hidden[e, a][:]),
+                in1=gates[:, e * C : (e + 1) * C].rearrange("p (c i) -> p c i", i=4).unsqueeze(2).to_broadcast([P, C // 4, PACK, 4]),
+                op=MULT,
+            )
+            return g
+
+        def quantised(e, a, g):
+            cq = keep.tile([P, C], U32, align_bytes=64, name="c_codes%d%d" % (e, a))
+            cs = keep.tile([P, C], U8, align_bytes=64, name="c_scales%d%d" % (e, a))
+            nc.vector.quantize_mx(out=cq[:].bitcast(FP8X4), scales=cs[:], in_=g[:].rearrange("p n t -> p (n t)"))
+            return cq, cs
+
+        def project(e, operands):
+            acc = psum2.tile([P, C], F32, name="acc")
+            for a in range(PASSES):
+                cq, cs = operands[a]
+                nc.tensor.matmul_mx(
+                    out=acc[:],
+                    lhsT=wp_codes[:, a * M : (a + 1) * M].bitcast(FP8X4),
+                    lhsT_scale=wp_scales[:, a * M : (a + 1) * M],
+                    rhs=cq[:].bitcast(FP8X4),
+                    rhs_scale=cs[:],
+                    start=(a == 0),
+                    stop=(a == PASSES - 1),
+                )
+            proj = keep.tile([P, C], F32, name="proj%d" % e)
+            nc.scalar.copy(out=proj[:], in_=acc[:])
+            return proj
+
+        def scatter(e, proj):
+            nc.vector.tensor_copy(result[:].indirect(offsets[:, e * C // 16 : (e + 1) * C // 16]), proj[:])
+
+        g00 = gated(0, 0)
+        g01 = gated(0, 1)
+        nc.vector.quantize_mx(
+            out=wp_codes[:].bitcast(FP8X4), scales=wp_scales[:], in_=wp_bf[:].rearrange("p a f t -> p (a f t)")
+        )
+        q00 = quantised(0, 0, g00)
+        q01 = quantised(0, 1, g01)
+        p0 = project(0, (q00, q01))
+        g10 = gated(1, 0)
+        g11 = gated(1, 1)
+        q10 = quantised(1, 0, g10)
+        q11 = quantised(1, 1, g11)
+        p1 = project(1, (q10, q11))
+        scatter(0, p0)
+        scatter(1, p1)
+        nc.sync.dma_start(out=out, in_=result[:])

@@ -37,9 +37,10 @@ def tile_moe_nxt_lin_relu_kernel(tc, xT, w_words, w_scales, b, wp, gate, offs, o
         s_perm = keep.tile([P, E, N], U8, align_bytes=64, name="s_perm")
         codes = keep.tile([P, T], U32, align_bytes=64, name="codes")
         scales = keep.tile([P, T], U8, align_bytes=64, name="scales")
-        bias = keep.tile([P, PASSES, PACK, E], F32, name="bias")
+        bias = [keep.tile([P, PACK, E], F32, align_bytes=64, tag="bias%d" % a, name="bias%d" % a) for a in range(PASSES)]
+        hidden_all = keep.tile([P, E * PASSES * PACK * C], F32, name="hidden")
         gates = keep.tile([P, E * C], F32, name="gates")
-        wp_raw = keep.tile([P, PASSES, PACK, M], F32, name="wp_raw")
+        wp_raw = hidden_all[:, 0 : PASSES * PACK * C].rearrange("p (a t f) -> p a t f", a=PASSES, t=PACK)[:, :, :, 0:M]
         wp_bf = keep.tile([P, PASSES, M, PACK], BF16, align_bytes=64, name="wp_bf")
         wp_codes = keep.tile([P, PASSES * M], U32, align_bytes=64, name="wp_codes")
         wp_scales = keep.tile([P, PASSES * M], U8, align_bytes=64, name="wp_scales")
@@ -49,9 +50,6 @@ def tile_moe_nxt_lin_relu_kernel(tc, xT, w_words, w_scales, b, wp, gate, offs, o
         nc.vector.memset(scales[:].bitcast(I32), 0)
         nc.vector.memset(result[:], 0.0)
         b_rows = b.rearrange("(a h t i) e -> a i h t e", a=PASSES, t=PACK, i=2)
-        for a in range(PASSES):
-            for i in range(2):
-                nc.gpsimd.dma_start(out=bias[i:P:2, a, :, :], in_=b_rows[a, i])
         wp_rows = wp.rearrange("(a h t i) f -> a i h t f", a=PASSES, t=PACK, i=2)
         x_rows = xT.rearrange("(p j) t -> p j t", j=PACK)
         chunks = [(0, 256, 96), (256, 256, 96), (512, 128, 48)]
@@ -74,13 +72,21 @@ def tile_moe_nxt_lin_relu_kernel(tc, xT, w_words, w_scales, b, wp, gate, offs, o
         for a in range(PASSES):
             for i in range(2):
                 nc.sync.dma_start(out=wp_raw[i:P:2, a, :, :], in_=wp_rows[a, i])
+
+        def load_bias(a):
+            for i in range(2):
+                nc.sync.dma_start(out=bias[a][i:P:2, :, :], in_=b_rows[a, i])
+
         load_words(1)
         nc.sync.dma_start(out=gates[:], in_=gate[0:P, :])
+        load_bias(0)
+        load_bias(1)
 
         def permute(engine, dst, src, dt):
+            line = 4 if dt == I32 else 8
             engine.tensor_copy(
-                out=dst.bitcast(dt).rearrange("p (a t h) -> p a t h", a=PASSES, t=PACK),
-                in_=src.bitcast(dt).rearrange("p (a h t) -> p a t h", a=PASSES, t=PACK),
+                out=dst.bitcast(dt).rearrange("p (a t g h) -> p a g t h", a=PASSES, t=PACK, h=line),
+                in_=src.bitcast(dt).rearrange("p (a g h t) -> p a g t h", a=PASSES, t=PACK, h=line),
             )
 
         permute(nc.vector, w_perm[:, 0, :], w_raw[:, 0, :], I32)
@@ -104,9 +110,7 @@ def tile_moe_nxt_lin_relu_kernel(tc, xT, w_words, w_scales, b, wp, gate, offs, o
             )
 
         for a in range(PASSES):
-            nc.gpsimd.tensor_scalar(
-                out=four(wp_bf[:, a]), in0=four_in(wp_raw[:, a]), scalar1=1.0, scalar2=0.0, op0=MULT, op1=ADD
-            )
+            nc.scalar.copy(out=four(wp_bf[:, a]), in_=four_in(wp_raw[:, a]))
 
         slot_codes = []
         slot_scales = []
@@ -124,39 +128,35 @@ def tile_moe_nxt_lin_relu_kernel(tc, xT, w_words, w_scales, b, wp, gate, offs, o
         hidden = {}
         for e in range(E):
             for a in range(PASSES):
-                h = keep.tile([P, PACK, C], F32, name="hidden%d%d" % (e, a))
+                h0 = (e * PASSES + a) * PACK * C
+                h = hidden_all[:, h0 : h0 + PACK * C].rearrange("p (t c) -> p t c", t=PACK)
                 hidden[e, a] = h
-                for half in range(2):
-                    bank = psum1.tile([P, 2, C], F32, name="bank")
-                    for i in range(2):
-                        t = 2 * half + i
-                        c0 = (a * PACK + t) * P
-                        nc.tensor.matmul_mx(
-                            out=bank[:, i, :],
-                            lhsT=w_perm[:, e, 2 * c0 : 2 * (c0 + P)].bitcast(FP4X4),
-                            lhsT_scale=s_perm[:, e, c0 : c0 + P],
-                            rhs=slot_codes[e][:].bitcast(FP8X4),
-                            rhs_scale=slot_scales[e][:],
-                            start=True,
-                            stop=True,
-                        )
-                        own_bias = bias[:, a, t, e : e + 1]
-                        nc.scalar.activation(out=h[:, t, :], in_=bank[:, i, :], func=RELU, bias=own_bias)
+                for t in range(PACK):
+                    bank = psum1.tile([P, C], F32, name="bank")
+                    c0 = (a * PACK + t) * P
+                    nc.tensor.matmul_mx(
+                        out=bank[:],
+                        lhsT=w_perm[:, e, 2 * c0 : 2 * (c0 + P)].bitcast(FP4X4),
+                        lhsT_scale=s_perm[:, e, c0 : c0 + P],
+                        rhs=slot_codes[e][:].bitcast(FP8X4),
+                        rhs_scale=slot_scales[e][:],
+                        start=True,
+                        stop=True,
+                    )
+                    nc.scalar.activation(out=h[:, t, :], in_=bank[:], func=RELU, bias=bias[a][:, t, e : e + 1])
 
-        def gated(e, a):
-            g = keep.tile([P, C, PACK], BF16, align_bytes=64, name="gated%d%d" % (e, a))
+        def gated(e, a, g):
             nc.vector.tensor_tensor(
-                out=four(g[:]),
-                in0=four_in(hidden[e, a][:]),
+                out=four(g),
+                in0=four_in(hidden[e, a]),
                 in1=gates[:, e * C : (e + 1) * C].rearrange("p (c i) -> p c i", i=4).unsqueeze(2).to_broadcast([P, C // 4, PACK, 4]),
                 op=MULT,
             )
-            return g
 
-        def quantised(e, a, g):
-            cq = keep.tile([P, C], U32, align_bytes=64, name="c_codes%d%d" % (e, a))
-            cs = keep.tile([P, C], U8, align_bytes=64, name="c_scales%d%d" % (e, a))
-            nc.vector.quantize_mx(out=cq[:].bitcast(FP8X4), scales=cs[:], in_=g[:].rearrange("p n t -> p (n t)"))
+        def quantised(name, tag, g, width):
+            cq = keep.tile([P, width], U32, align_bytes=64, tag=tag, name="c_codes" + name)
+            cs = keep.tile([P, width], U8, align_bytes=64, name="c_scales" + name)
+            nc.vector.quantize_mx(out=cq[:].bitcast(FP8X4), scales=cs[:], in_=g)
             return cq, cs
 
         def project(e, operands):
@@ -167,8 +167,8 @@ def tile_moe_nxt_lin_relu_kernel(tc, xT, w_words, w_scales, b, wp, gate, offs, o
                     out=acc[:],
                     lhsT=wp_codes[:, a * M : (a + 1) * M].bitcast(FP8X4),
                     lhsT_scale=wp_scales[:, a * M : (a + 1) * M],
-                    rhs=cq[:].bitcast(FP8X4),
-                    rhs_scale=cs[:],
+                    rhs=cq.bitcast(FP8X4),
+                    rhs_scale=cs,
                     start=(a == 0),
                     stop=(a == PASSES - 1),
                 )
@@ -179,19 +179,20 @@ def tile_moe_nxt_lin_relu_kernel(tc, xT, w_words, w_scales, b, wp, gate, offs, o
         def scatter(e, proj):
             nc.vector.tensor_copy(result[:].indirect(offsets[:, e * C // 16 : (e + 1) * C // 16]), proj[:])
 
-        g00 = gated(0, 0)
-        g01 = gated(0, 1)
+        g0 = keep.tile([P, PASSES, C, PACK], BF16, align_bytes=64, name="gated0")
+        g1 = keep.tile([P, PASSES, C, PACK], BF16, align_bytes=64, name="gated1")
         nc.vector.quantize_mx(
             out=wp_codes[:].bitcast(FP8X4), scales=wp_scales[:], in_=wp_bf[:].rearrange("p a f t -> p (a f t)")
         )
-        q00 = quantised(0, 0, g00)
-        q01 = quantised(0, 1, g01)
-        p0 = project(0, (q00, q01))
-        g10 = gated(1, 0)
-        g11 = gated(1, 1)
-        q10 = quantised(1, 0, g10)
-        q11 = quantised(1, 1, g11)
-        p1 = project(1, (q10, q11))
+        gated(0, 0, g0[:, 0])
+        gated(0, 1, g0[:, 1])
+        gated(1, 0, g1[:, 0])
+        q0, s0 = quantised("0", "bias0", g0[:].rearrange("p a n t -> p (a n t)"), PASSES * C)
+        p0 = project(0, [(q0[:, a * C : (a + 1) * C], s0[:, a * C : (a + 1) * C]) for a in range(PASSES)])
+        gated(1, 1, g1[:, 1])
+        q10, s10 = quantised("10", "bias1", g1[:, 0].rearrange("p n t -> p (n t)"), C)
+        q11, s11 = quantised("11", "c_codes11", g1[:, 1].rearrange("p n t -> p (n t)"), C)
+        p1 = project(1, [(q10[:], s10[:]), (q11[:], s11[:])])
         scatter(0, p0)
         scatter(1, p1)
         nc.sync.dma_start(out=out, in_=result[:])

@@ -60,14 +60,19 @@ def tile_moe_nxt_lin_relu_kernel(tc, xT, w_words, w_scales, b, wp, gate, offs, o
         def load_words(e):
             nc.sync.dma_start(out=w_raw[:, e, :].bitcast(I32), in_=w_words[e, 0].bitcast(I32))
 
-        load_words(0)
+        def load_tokens(n):
+            t0, width, cut = chunks[n]
+            nc.sync.dma_start(out=x_raw[n][:], in_=x_rows[:, :, t0 : t0 + width])
+
+        load_tokens(0)
         for q in range(4):
             nc.sync.dma_start(
                 out=s_raw[32 * q : 32 * q + 4, :, :].bitcast(I32),
                 in_=w_scales[:, 0, 4 * q : 4 * q + 4, :].rearrange("e q n -> q e n").bitcast(I32),
             )
-        for (t0, width, cut), raw in zip(chunks, x_raw):
-            nc.sync.dma_start(out=raw[:], in_=x_rows[:, :, t0 : t0 + width])
+        load_tokens(1)
+        load_tokens(2)
+        load_words(0)
         nc.sync.dma_start(offsets[:], offs)
         for a in range(PASSES):
             for i in range(2):

@@ -31,16 +31,16 @@ def tile_moe_nxt_lin_relu_kernel(tc, xT, w_words, w_scales, b, wp, gate, offs, o
         psum2 = ctx.enter_context(tc.psum_pool(name="psum2", bufs=2))
 
         offsets = keep.tile([P, E * C // 16], U16, name="offsets")
-        w_raw = keep.tile([P, E, 2 * N], U8, align_bytes=64, name="w_raw")
+        w_raw = [keep.tile([P, 2 * N], U8, align_bytes=64, tag="w_raw%d" % e, name="w_raw%d" % e) for e in range(E)]
         w_perm = keep.tile([P, E, 2 * N], U8, align_bytes=64, name="w_perm")
         s_raw = keep.tile([P, E, N], U8, align_bytes=64, name="s_raw")
         s_perm = keep.tile([P, E, N], U8, align_bytes=64, name="s_perm")
         codes = keep.tile([P, T], U32, align_bytes=64, name="codes")
         scales = keep.tile([P, T], U8, align_bytes=64, name="scales")
-        bias = [keep.tile([P, PACK, E], F32, align_bytes=64, tag="bias%d" % a, name="bias%d" % a) for a in range(PASSES)]
+        bias_raw = keep.tile([P, PASSES, PACK, E], F32, name="bias_raw")
         hidden_all = keep.tile([P, E * PASSES * PACK * C], F32, name="hidden")
         gates = keep.tile([P, E * C], F32, name="gates")
-        wp_raw = hidden_all[:, 0 : PASSES * PACK * C].rearrange("p (a t f) -> p a t f", a=PASSES, t=PACK)[:, :, :, 0:M]
+        wp_raw = keep.tile([P, PASSES, PACK, M], F32, align_bytes=64, tag="bias0", name="wp_raw")
         wp_bf = keep.tile([P, PASSES, M, PACK], BF16, align_bytes=64, name="wp_bf")
         wp_codes = keep.tile([P, PASSES * M], U32, align_bytes=64, name="wp_codes")
         wp_scales = keep.tile([P, PASSES * M], U8, align_bytes=64, name="wp_scales")
@@ -58,7 +58,7 @@ def tile_moe_nxt_lin_relu_kernel(tc, xT, w_words, w_scales, b, wp, gate, offs, o
             x_raw.append(keep.tile([P, PACK, width], F32, name="x_raw%d" % t0))
 
         def load_words(e):
-            nc.sync.dma_start(out=w_raw[:, e, :].bitcast(I32), in_=w_words[e, 0].bitcast(I32))
+            nc.sync.dma_start(out=w_raw[e][:].bitcast(I32), in_=w_words[e, 0].bitcast(I32))
 
         def load_tokens(n):
             t0, width, cut = chunks[n]
@@ -74,18 +74,18 @@ def tile_moe_nxt_lin_relu_kernel(tc, xT, w_words, w_scales, b, wp, gate, offs, o
         load_tokens(2)
         load_words(0)
         nc.sync.dma_start(offsets[:], offs)
-        for a in range(PASSES):
-            for i in range(2):
-                nc.sync.dma_start(out=wp_raw[i:P:2, a, :, :], in_=wp_rows[a, i])
 
         def load_bias(a):
             for i in range(2):
-                nc.sync.dma_start(out=bias[a][i:P:2, :, :], in_=b_rows[a, i])
+                nc.sync.dma_start(out=bias_raw[i:P:2, a, :, :], in_=b_rows[a, i])
 
-        load_words(1)
-        nc.sync.dma_start(out=gates[:], in_=gate[0:P, :])
+        for a in range(PASSES):
+            for i in range(2):
+                nc.sync.dma_start(out=wp_raw[i:P:2, a, :, :], in_=wp_rows[a, i])
         load_bias(0)
         load_bias(1)
+        load_words(1)
+        nc.sync.dma_start(out=gates[:], in_=gate[0:P, :])
 
         def permute(engine, dst, src, dt):
             line = 4 if dt == I32 else 8
@@ -94,7 +94,7 @@ def tile_moe_nxt_lin_relu_kernel(tc, xT, w_words, w_scales, b, wp, gate, offs, o
                 in_=src.bitcast(dt).rearrange("p (a g h t) -> p a g t h", a=PASSES, t=PACK, h=line),
             )
 
-        permute(nc.vector, w_perm[:, 0, :], w_raw[:, 0, :], I32)
+        permute(nc.vector, w_perm[:, 0, :], w_raw[0][:], I32)
         for e in range(E):
             permute(nc.vector, s_perm[:, e, :], s_raw[:, e, :], U16)
 
@@ -116,6 +116,11 @@ def tile_moe_nxt_lin_relu_kernel(tc, xT, w_words, w_scales, b, wp, gate, offs, o
 
         for a in range(PASSES):
             nc.scalar.copy(out=four(wp_bf[:, a]), in_=four_in(wp_raw[:, a]))
+        bias_both = keep.tile([P, PASSES, PACK, E], F32, align_bytes=64, tag="bias0", name="bias_both")
+        nc.scalar.copy(out=bias_both[:], in_=bias_raw[:])
+        bias1 = keep.tile([P, PACK, E], F32, align_bytes=64, tag="bias1", name="bias1")
+        nc.gpsimd.tensor_copy(out=bias1[:], in_=bias_both[:, 1])
+        bias = (bias_both[:, 0], bias1)
 
         slot_codes = []
         slot_scales = []
@@ -128,7 +133,7 @@ def tile_moe_nxt_lin_relu_kernel(tc, xT, w_words, w_scales, b, wp, gate, offs, o
             slot_codes.append(sc)
             slot_scales.append(ss)
 
-        permute(nc.vector, w_perm[:, 1, :], w_raw[:, 1, :], I32)
+        permute(nc.vector, w_perm[:, 1, :], w_raw[1][:], I32)
 
         hidden = {}
         for e in range(E):
@@ -184,7 +189,7 @@ def tile_moe_nxt_lin_relu_kernel(tc, xT, w_words, w_scales, b, wp, gate, offs, o
         def scatter(e, proj):
             nc.vector.tensor_copy(result[:].indirect(offsets[:, e * C // 16 : (e + 1) * C // 16]), proj[:])
 
-        g0 = keep.tile([P, PASSES, C, PACK], BF16, align_bytes=64, name="gated0")
+        g0 = keep.tile([P, PASSES, C, PACK], BF16, align_bytes=64, tag="w_raw1", name="gated0")
         g1 = keep.tile([P, PASSES, C, PACK], BF16, align_bytes=64, name="gated1")
         nc.vector.quantize_mx(
             out=wp_codes[:].bitcast(FP8X4), scales=wp_scales[:], in_=wp_bf[:].rearrange("p a f t -> p (a f t)")

@@ -1,11 +1,13 @@
 from contextlib import ExitStack
 
 import concourse.mybir as mybir
+from concourse.masks import make_identity
 
 K, T, E, C, N, M = 512, 640, 2, 256, 1024, 128
 P = 128
 PACK = 4
 PASSES = N // 512
+SHARE = 64
 
 FLOPS = 2 * E * C * K * N + 2 * E * C * N * M
 BYTES = 4 * K * T + E * K * N // 2 + E * K * N // 32 + 4 * N * E + 4 * N * M + 4 * E * C + 2 * P * (E * C // 16) + 4 * M * T
@@ -28,7 +30,7 @@ def tile_moe_nxt_lin_relu_kernel(tc, xT, w_words, w_scales, b, wp, gate, offs, o
     with ExitStack() as ctx:
         keep = ctx.enter_context(tc.tile_pool(name="keep", bufs=1))
         psum1 = ctx.enter_context(tc.psum_pool(name="psum1", bufs=6))
-        psum2 = ctx.enter_context(tc.psum_pool(name="psum2", bufs=2))
+        psum2 = ctx.enter_context(tc.psum_pool(name="psum2", bufs=1))
 
         offsets = keep.tile([P, E * C // 16], U16, name="offsets")
         w_raw = [keep.tile([P, 2 * N], U8, align_bytes=64, tag="w_raw%d" % e, name="w_raw%d" % e) for e in range(E)]
@@ -39,7 +41,14 @@ def tile_moe_nxt_lin_relu_kernel(tc, xT, w_words, w_scales, b, wp, gate, offs, o
         scales = keep.tile([P, T], U8, align_bytes=64, name="scales")
         bias_raw = keep.tile([P, PASSES, PACK, E], F32, name="bias_raw")
         hidden_all = keep.tile([P, E * PASSES * PACK * C], F32, name="hidden")
-        gates = keep.tile([P, E * C], F32, name="gates")
+        gate_cols = keep.tile([P, E * C // P], F32, name="gate_cols")
+        gates_sb = keep.tile([P, E, SHARE], F32, name="gates_sb")
+        identity = keep.tile([P, P], F32, name="identity")
+        gates = psum2.tile([P, E * C], F32, name="gates")
+        gate_rows = keep.tile([P, P], F32, name="gate_rows")
+        accs = psum2.tile([P, E, C], F32, name="accs")
+        nc.gpsimd.memset(gate_rows[:], 0.0)
+        make_identity(nc, identity[:])
         wp_raw = keep.tile([P, PASSES, PACK, M], F32, align_bytes=64, tag="bias0", name="wp_raw")
         wp_bf = keep.tile([P, PASSES, M, PACK], BF16, align_bytes=64, name="wp_bf")
         wp_codes = keep.tile([P, PASSES * M], U32, align_bytes=64, name="wp_codes")
@@ -70,6 +79,7 @@ def tile_moe_nxt_lin_relu_kernel(tc, xT, w_words, w_scales, b, wp, gate, offs, o
                 out=s_raw[32 * q : 32 * q + 4, :, :].bitcast(I32),
                 in_=w_scales[:, 0, 4 * q : 4 * q + 4, :].rearrange("e q n -> q e n").bitcast(I32),
             )
+        nc.sync.dma_start(out=gate_rows[0 : E * C // P, :], in_=gate[0, :].rearrange("(c p) -> c p", p=P))
         load_tokens(1)
         load_tokens(2)
         load_words(0)
@@ -85,7 +95,12 @@ def tile_moe_nxt_lin_relu_kernel(tc, xT, w_words, w_scales, b, wp, gate, offs, o
         load_bias(0)
         load_bias(1)
         load_words(1)
-        nc.sync.dma_start(out=gates[:], in_=gate[0:P, :])
+
+        nc.tensor.transpose(accs[:, 0, 0:P], gate_rows[:], identity[:])
+        nc.scalar.copy(out=gate_cols[:], in_=accs[:, 0, 0 : E * C // P])
+        for c in range(E * C // P):
+            nc.tensor.transpose(gates[:, c * P : (c + 1) * P], gate_cols[:, c : c + 1].to_broadcast([P, P]), identity[:])
+        nc.scalar.copy(out=gates_sb[:], in_=gates[:].rearrange("p (e c) -> p e c", e=E)[:, :, 0:SHARE])
 
         def permute(engine, dst, src, dt):
             line = 4 if dt == I32 else 8
@@ -118,9 +133,11 @@ def tile_moe_nxt_lin_relu_kernel(tc, xT, w_words, w_scales, b, wp, gate, offs, o
             nc.scalar.copy(out=four(wp_bf[:, a]), in_=four_in(wp_raw[:, a]))
         bias_both = keep.tile([P, PASSES, PACK, E], F32, align_bytes=64, tag="bias0", name="bias_both")
         nc.scalar.copy(out=bias_both[:], in_=bias_raw[:])
-        bias1 = keep.tile([P, PACK, E], F32, align_bytes=64, tag="bias1", name="bias1")
-        nc.gpsimd.tensor_copy(out=bias1[:], in_=bias_both[:, 1])
-        bias = (bias_both[:, 0], bias1)
+        bias = {(0, 0): bias_both[:, 0, :, 0]}
+        for e, a in ((0, 1), (1, 0), (1, 1)):
+            own = keep.tile([P, PACK], F32, align_bytes=64, tag="bias%d%d" % (e, a), name="bias%d%d" % (e, a))
+            nc.gpsimd.tensor_copy(out=own[:], in_=bias_both[:, a, :, e])
+            bias[e, a] = own
 
         slot_codes = []
         slot_scales = []
@@ -153,13 +170,22 @@ def tile_moe_nxt_lin_relu_kernel(tc, xT, w_words, w_scales, b, wp, gate, offs, o
                         start=True,
                         stop=True,
                     )
-                    nc.scalar.activation(out=h[:, t, :], in_=bank[:], func=RELU, bias=bias[a][:, t, e : e + 1])
+                    nc.scalar.activation(out=h[:, t, :], in_=bank[:], func=RELU, bias=bias[e, a][:, t : t + 1])
 
         def gated(e, a, g):
+            nc.gpsimd.tensor_tensor(
+                out=g[:, 0:SHARE, :].rearrange("p (c i) t -> p c t i", i=2),
+                in0=hidden[e, a][:, :, 0:SHARE].rearrange("p t (c i) -> p c t i", i=2),
+                in1=gates_sb[:, e, :].rearrange("p (c i) -> p c i", i=2).unsqueeze(2).to_broadcast([P, SHARE // 2, PACK, 2]),
+                op=MULT,
+            )
             nc.vector.tensor_tensor(
-                out=four(g),
-                in0=four_in(hidden[e, a]),
-                in1=gates[:, e * C : (e + 1) * C].rearrange("p (c i) -> p c i", i=4).unsqueeze(2).to_broadcast([P, C // 4, PACK, 4]),
+                out=four(g[:, SHARE:C, :]),
+                in0=four_in(hidden[e, a][:, :, SHARE:C]),
+                in1=gates[:, e * C + SHARE : (e + 1) * C]
+                .rearrange("p (c i) -> p c i", i=4)
+                .unsqueeze(2)
+                .to_broadcast([P, (C - SHARE) // 4, PACK, 4]),
                 op=MULT,
             )
 
@@ -170,11 +196,11 @@ def tile_moe_nxt_lin_relu_kernel(tc, xT, w_words, w_scales, b, wp, gate, offs, o
             return cq, cs
 
         def project(e, operands):
-            acc = psum2.tile([P, C], F32, name="acc")
+            acc = accs[:, e, :]
             for a in range(PASSES):
                 cq, cs = operands[a]
                 nc.tensor.matmul_mx(
-                    out=acc[:],
+                    out=acc,
                     lhsT=wp_codes[:, a * M : (a + 1) * M].bitcast(FP8X4),
                     lhsT_scale=wp_scales[:, a * M : (a + 1) * M],
                     rhs=cq.bitcast(FP8X4),
@@ -183,7 +209,7 @@ def tile_moe_nxt_lin_relu_kernel(tc, xT, w_words, w_scales, b, wp, gate, offs, o
                     stop=(a == PASSES - 1),
                 )
             proj = keep.tile([P, C], F32, name="proj%d" % e)
-            nc.scalar.copy(out=proj[:], in_=acc[:])
+            nc.scalar.copy(out=proj[:], in_=acc)
             return proj
 
         def scatter(e, proj):
@@ -196,11 +222,12 @@ def tile_moe_nxt_lin_relu_kernel(tc, xT, w_words, w_scales, b, wp, gate, offs, o
         )
         gated(0, 0, g0[:, 0])
         gated(0, 1, g0[:, 1])
+        q00, s00 = quantised("00", "bias01", g0[:, 0].rearrange("p n t -> p (n t)"), C)
         gated(1, 0, g1[:, 0])
-        q0, s0 = quantised("0", "bias0", g0[:].rearrange("p a n t -> p (a n t)"), PASSES * C)
-        p0 = project(0, [(q0[:, a * C : (a + 1) * C], s0[:, a * C : (a + 1) * C]) for a in range(PASSES)])
+        q01, s01 = quantised("01", "bias10", g0[:, 1].rearrange("p n t -> p (n t)"), C)
+        p0 = project(0, [(q00[:], s00[:]), (q01[:], s01[:])])
         gated(1, 1, g1[:, 1])
-        q10, s10 = quantised("10", "bias1", g1[:, 0].rearrange("p n t -> p (n t)"), C)
+        q10, s10 = quantised("10", "bias11", g1[:, 0].rearrange("p n t -> p (n t)"), C)
         q11, s11 = quantised("11", "c_codes11", g1[:, 1].rearrange("p n t -> p (n t)"), C)
         p1 = project(1, [(q10[:], s10[:]), (q11[:], s11[:])])
         scatter(0, p0)

@@ -8,6 +8,7 @@ P = 128
 PACK = 4
 PASSES = N // 512
 SHARE = 64
+HALF = C // 2
 
 FLOPS = 2 * E * C * K * N + 2 * E * C * N * M
 BYTES = 4 * K * T + E * K * N // 2 + E * K * N // 32 + 4 * N * E + 4 * N * M + 4 * E * C + 2 * P * (E * C // 16) + 4 * M * T
@@ -39,26 +40,22 @@ def tile_moe_nxt_lin_relu_kernel(tc, xT, w_words, w_scales, b, wp, gate, offs, o
         s_perm = keep.tile([P, E, N], U8, align_bytes=64, name="s_perm")
         codes = keep.tile([P, T], U32, align_bytes=64, name="codes")
         scales = keep.tile([P, T], U8, align_bytes=64, name="scales")
-        bias_raw = keep.tile([P, PASSES, PACK, E], F32, name="bias_raw")
-        hidden_all = keep.tile([P, E * PASSES * PACK * C], F32, name="hidden")
-        gate_cols = keep.tile([P, E * C // P], F32, name="gate_cols")
+        bias_raw = keep.tile([P, PASSES, 16], F32, name="bias_raw")
+        gate_cols = keep.tile([P, PACK], F32, name="gate_cols")
         gates_sb = keep.tile([P, E, SHARE], F32, name="gates_sb")
         identity = keep.tile([P, P], F32, name="identity")
-        gates = psum2.tile([P, E * C], F32, name="gates")
-        gate_rows = keep.tile([P, P], F32, name="gate_rows")
+        gates = psum2.tile([P, P, PACK], F32, name="gates")
         accs = psum2.tile([P, E, C], F32, name="accs")
-        nc.gpsimd.memset(gate_rows[:], 0.0)
         make_identity(nc, identity[:])
-        wp_raw = keep.tile([P, PASSES, PACK, M], F32, align_bytes=64, tag="bias0", name="wp_raw")
+        wp_raw = [keep.tile([P, PACK, M], F32, name="wp_raw%d" % a) for a in range(PASSES)]
         wp_bf = keep.tile([P, PASSES, M, PACK], BF16, align_bytes=64, name="wp_bf")
-        wp_codes = keep.tile([P, PASSES * M], U32, align_bytes=64, name="wp_codes")
         wp_scales = keep.tile([P, PASSES * M], U8, align_bytes=64, name="wp_scales")
         result = keep.tile([P, T], F32, name="result")
 
         nc.vector.memset(s_raw[:].rearrange("p e n -> p (e n)").bitcast(I32), 0)
         nc.vector.memset(scales[:].bitcast(I32), 0)
         nc.vector.memset(result[:], 0.0)
-        b_rows = b.rearrange("(a h t i) e -> a i h t e", a=PASSES, t=PACK, i=2)
+        b_runs = b.rearrange("(a h r) e -> h a (r e)", a=PASSES, r=8)
         wp_rows = wp.rearrange("(a h t i) f -> a i h t f", a=PASSES, t=PACK, i=2)
         x_rows = xT.rearrange("(p j) t -> p j t", j=PACK)
         chunks = [(0, 256, 96), (256, 256, 96), (512, 128, 48)]
@@ -73,34 +70,33 @@ def tile_moe_nxt_lin_relu_kernel(tc, xT, w_words, w_scales, b, wp, gate, offs, o
             t0, width, cut = chunks[n]
             nc.sync.dma_start(out=x_raw[n][:], in_=x_rows[:, :, t0 : t0 + width])
 
+        nc.sync.dma_start(out=gate_cols[:], in_=gate[0, :].rearrange("(p i) -> p i", i=PACK))
         load_tokens(0)
         for q in range(4):
             nc.sync.dma_start(
                 out=s_raw[32 * q : 32 * q + 4, :, :].bitcast(I32),
                 in_=w_scales[:, 0, 4 * q : 4 * q + 4, :].rearrange("e q n -> q e n").bitcast(I32),
             )
-        nc.sync.dma_start(out=gate_rows[0 : E * C // P, :], in_=gate[0, :].rearrange("(c p) -> c p", p=P))
         load_tokens(1)
         load_tokens(2)
         load_words(0)
         nc.sync.dma_start(offsets[:], offs)
 
-        def load_bias(a):
-            for i in range(2):
-                nc.sync.dma_start(out=bias_raw[i:P:2, a, :, :], in_=b_rows[a, i])
 
-        for a in range(PASSES):
+        def load_wp(a):
             for i in range(2):
-                nc.sync.dma_start(out=wp_raw[i:P:2, a, :, :], in_=wp_rows[a, i])
-        load_bias(0)
-        load_bias(1)
+                nc.sync.dma_start(out=wp_raw[a][i:P:2, :, :], in_=wp_rows[a, i])
+
+        load_wp(0)
+        for i in range(2):
+            nc.sync.dma_start(out=bias_raw[i:P:2, :, 0:14], in_=b_runs[:, :, 2 * i : 2 * i + 14])
         load_words(1)
+        load_wp(1)
 
-        nc.tensor.transpose(accs[:, 0, 0:P], gate_rows[:], identity[:])
-        nc.scalar.copy(out=gate_cols[:], in_=accs[:, 0, 0 : E * C // P])
-        for c in range(E * C // P):
-            nc.tensor.transpose(gates[:, c * P : (c + 1) * P], gate_cols[:, c : c + 1].to_broadcast([P, P]), identity[:])
-        nc.scalar.copy(out=gates_sb[:], in_=gates[:].rearrange("p (e c) -> p e c", e=E)[:, :, 0:SHARE])
+        for i in range(PACK):
+            nc.tensor.transpose(gates[:, :, i], gate_cols[:, i : i + 1].to_broadcast([P, P]), identity[:])
+        by_slot = gates[:].rearrange("p (e g) i -> p e g i", e=E)
+        nc.scalar.copy(out=gates_sb[:].rearrange("p e (g i) -> p e g i", i=PACK), in_=by_slot[:, :, 0 : SHARE // PACK, :])
 
         def permute(engine, dst, src, dt):
             line = 4 if dt == I32 else 8
@@ -129,70 +125,76 @@ def tile_moe_nxt_lin_relu_kernel(tc, xT, w_words, w_scales, b, wp, gate, offs, o
                 in_=grouped[:].rearrange("p t j -> p (t j)"),
             )
 
-        for a in range(PASSES):
-            nc.scalar.copy(out=four(wp_bf[:, a]), in_=four_in(wp_raw[:, a]))
-        bias_both = keep.tile([P, PASSES, PACK, E], F32, align_bytes=64, tag="bias0", name="bias_both")
-        nc.scalar.copy(out=bias_both[:], in_=bias_raw[:])
-        bias = {(0, 0): bias_both[:, 0, :, 0]}
+        nc.scalar.copy(out=four(wp_bf[:, 0]), in_=four_in(wp_raw[0][:]))
+        bias_own = bias_raw[:].rearrange("p a (t r) -> p a t r", t=PACK)
+        bias = {(0, 0): bias_own[:, 0, :, 0]}
         for e, a in ((0, 1), (1, 0), (1, 1)):
             own = keep.tile([P, PACK], F32, align_bytes=64, tag="bias%d%d" % (e, a), name="bias%d%d" % (e, a))
-            nc.gpsimd.tensor_copy(out=own[:], in_=bias_both[:, a, :, e])
+            nc.scalar.copy(out=own[:], in_=bias_own[:, a, :, e])
             bias[e, a] = own
 
         slot_codes = []
         slot_scales = []
         for e in range(E):
-            own = offsets[:, e * C // 16 : (e + 1) * C // 16]
-            sc = keep.tile([P, C], U32, align_bytes=64, name="slot_codes%d" % e)
+            sc = keep.tile([P, C], U32, align_bytes=64, tag="slot_codes%d" % e, name="slot_codes%d" % e)
             ss = keep.tile([P, C], U8, align_bytes=64, name="slot_scales%d" % e)
-            nc.vector.tensor_copy(sc[:], codes[:].indirect(own))
-            nc.vector.tensor_copy(ss[:], scales[:].indirect(own))
+            for u0, u1 in ((0, HALF), (HALF, C)) if e == 0 else ((0, C),):
+                own = offsets[:, (e * C + u0) // 16 : (e * C + u1) // 16]
+                nc.vector.tensor_copy(sc[:, u0:u1], codes[:].indirect(own))
+                nc.vector.tensor_copy(ss[:, u0:u1], scales[:].indirect(own))
             slot_codes.append(sc)
             slot_scales.append(ss)
 
-        permute(nc.vector, w_perm[:, 1, :], w_raw[1][:], I32)
+        permute(nc.gpsimd, w_perm[:, 1, :], w_raw[1][:], I32)
+        nc.gpsimd.tensor_scalar(
+            out=four(wp_bf[:, 1]), in0=four_in(wp_raw[1][:]), scalar1=1.0, scalar2=0.0, op0=MULT, op1=ADD
+        )
 
-        hidden = {}
-        for e in range(E):
-            for a in range(PASSES):
-                h0 = (e * PASSES + a) * PACK * C
-                h = hidden_all[:, h0 : h0 + PACK * C].rearrange("p (t c) -> p t c", t=PACK)
-                hidden[e, a] = h
-                for t in range(PACK):
-                    bank = psum1.tile([P, C], F32, name="bank")
-                    c0 = (a * PACK + t) * P
-                    nc.tensor.matmul_mx(
-                        out=bank[:],
-                        lhsT=w_perm[:, e, 2 * c0 : 2 * (c0 + P)].bitcast(FP4X4),
-                        lhsT_scale=s_perm[:, e, c0 : c0 + P],
-                        rhs=slot_codes[e][:].bitcast(FP8X4),
-                        rhs_scale=slot_scales[e][:],
-                        start=True,
-                        stop=True,
-                    )
-                    nc.scalar.activation(out=h[:, t, :], in_=bank[:], func=RELU, bias=bias[e, a][:, t : t + 1])
+        def expert(e, a, u0, u1):
+            h = keep.tile([P, PACK, u1 - u0], F32, align_bytes=64, tag="hidden%d%d%d" % (e, a, u0), name="hidden%d%d%d" % (e, a, u0))
+            for t in range(PACK):
+                bank = psum1.tile([P, u1 - u0], F32, name="bank")
+                c0 = (a * PACK + t) * P
+                nc.tensor.matmul_mx(
+                    out=bank[:],
+                    lhsT=w_perm[:, e, 2 * c0 : 2 * (c0 + P)].bitcast(FP4X4),
+                    lhsT_scale=s_perm[:, e, c0 : c0 + P],
+                    rhs=slot_codes[e][:, u0:u1].bitcast(FP8X4),
+                    rhs_scale=slot_scales[e][:, u0:u1],
+                    start=True,
+                    stop=True,
+                )
+                nc.scalar.activation(out=h[:, t, :], in_=bank[:], func=RELU, bias=bias[e, a][:, t : t + 1])
+            return h
+
+        first = expert(0, 0, 0, HALF)
+        second = expert(0, 0, HALF, C)
+        hidden = {(e, a): expert(e, a, 0, C) for e, a in ((0, 1), (1, 0), (1, 1))}
+
+        def on_gpsimd(e, h, g, width):
+            nc.gpsimd.tensor_tensor(
+                out=g.rearrange("p (c i) t -> p c t i", i=2),
+                in0=h.rearrange("p t (c i) -> p c t i", i=2),
+                in1=gates_sb[:, e, 0:width].rearrange("p (c i) -> p c i", i=2).unsqueeze(2).to_broadcast([P, width // 2, PACK, 2]),
+                op=MULT,
+            )
+
+        def on_vector(e, h, g, u0, u1):
+            nc.vector.tensor_tensor(
+                out=four(g),
+                in0=four_in(h),
+                in1=by_slot[:, e, u0 // PACK : u1 // PACK, :].unsqueeze(2).to_broadcast([P, (u1 - u0) // 4, PACK, 4]),
+                op=MULT,
+            )
 
         def gated(e, a, g):
-            nc.gpsimd.tensor_tensor(
-                out=g[:, 0:SHARE, :].rearrange("p (c i) t -> p c t i", i=2),
-                in0=hidden[e, a][:, :, 0:SHARE].rearrange("p t (c i) -> p c t i", i=2),
-                in1=gates_sb[:, e, :].rearrange("p (c i) -> p c i", i=2).unsqueeze(2).to_broadcast([P, SHARE // 2, PACK, 2]),
-                op=MULT,
-            )
-            nc.vector.tensor_tensor(
-                out=four(g[:, SHARE:C, :]),
-                in0=four_in(hidden[e, a][:, :, SHARE:C]),
-                in1=gates[:, e * C + SHARE : (e + 1) * C]
-                .rearrange("p (c i) -> p c i", i=4)
-                .unsqueeze(2)
-                .to_broadcast([P, (C - SHARE) // 4, PACK, 4]),
-                op=MULT,
-            )
+            on_gpsimd(e, hidden[e, a][:, :, 0:SHARE], g[:, 0:SHARE, :], SHARE)
+            on_vector(e, hidden[e, a][:, :, SHARE:C], g[:, SHARE:C, :], SHARE, C)
 
         def quantised(name, tag, g, width):
             cq = keep.tile([P, width], U32, align_bytes=64, tag=tag, name="c_codes" + name)
             cs = keep.tile([P, width], U8, align_bytes=64, name="c_scales" + name)
-            nc.vector.quantize_mx(out=cq[:].bitcast(FP8X4), scales=cs[:], in_=g)
+            nc.vector.quantize_mx(out=cq[:].bitcast(FP8X4), scales=cs[:], in_=g.rearrange("p n t -> p (n t)"))
             return cq, cs
 
         def project(e, operands):
@@ -203,8 +205,8 @@ def tile_moe_nxt_lin_relu_kernel(tc, xT, w_words, w_scales, b, wp, gate, offs, o
                     out=acc,
                     lhsT=wp_codes[:, a * M : (a + 1) * M].bitcast(FP8X4),
                     lhsT_scale=wp_scales[:, a * M : (a + 1) * M],
-                    rhs=cq.bitcast(FP8X4),
-                    rhs_scale=cs,
+                    rhs=cq[:].bitcast(FP8X4),
+                    rhs_scale=cs[:],
                     start=(a == 0),
                     stop=(a == PASSES - 1),
                 )
@@ -215,21 +217,25 @@ def tile_moe_nxt_lin_relu_kernel(tc, xT, w_words, w_scales, b, wp, gate, offs, o
         def scatter(e, proj):
             nc.vector.tensor_copy(result[:].indirect(offsets[:, e * C // 16 : (e + 1) * C // 16]), proj[:])
 
-        g0 = keep.tile([P, PASSES, C, PACK], BF16, align_bytes=64, tag="w_raw1", name="gated0")
-        g1 = keep.tile([P, PASSES, C, PACK], BF16, align_bytes=64, name="gated1")
+        g00 = keep.tile([P, C, PACK], BF16, align_bytes=64, name="gated00")
+        g01 = keep.tile([P, C, PACK], BF16, align_bytes=64, name="gated01")
+        g10 = keep.tile([P, C, PACK], BF16, align_bytes=64, name="gated10")
+        g11 = keep.tile([P, C, PACK], BF16, align_bytes=64, name="gated11")
+        on_vector(0, first[:], g00[:, 0:HALF, :], 0, HALF)
+        on_vector(0, second[:], g00[:, HALF:C, :], HALF, C)
+        wp_codes = keep.tile([P, PASSES * M], U32, align_bytes=64, tag="hidden00128", name="wp_codes")
         nc.vector.quantize_mx(
             out=wp_codes[:].bitcast(FP8X4), scales=wp_scales[:], in_=wp_bf[:].rearrange("p a f t -> p (a f t)")
         )
-        gated(0, 0, g0[:, 0])
-        gated(0, 1, g0[:, 1])
-        q00, s00 = quantised("00", "bias01", g0[:, 0].rearrange("p n t -> p (n t)"), C)
-        gated(1, 0, g1[:, 0])
-        q01, s01 = quantised("01", "bias10", g0[:, 1].rearrange("p n t -> p (n t)"), C)
-        p0 = project(0, [(q00[:], s00[:]), (q01[:], s01[:])])
-        gated(1, 1, g1[:, 1])
-        q10, s10 = quantised("10", "bias11", g1[:, 0].rearrange("p n t -> p (n t)"), C)
-        q11, s11 = quantised("11", "c_codes11", g1[:, 1].rearrange("p n t -> p (n t)"), C)
-        p1 = project(1, [(q10[:], s10[:]), (q11[:], s11[:])])
+        gated(0, 1, g01)
+        q00 = quantised("00", "bias01", g00[:], C)
+        gated(1, 0, g10)
+        q01 = quantised("01", "bias10", g01[:], C)
+        gated(1, 1, g11)
+        q10 = quantised("10", "bias11", g10[:], C)
+        q11 = quantised("11", "c_codes11", g11[:], C)
+        p0 = project(0, [q00, q01])
+        p1 = project(1, [q10, q11])
         scatter(0, p0)
         scatter(1, p1)
         nc.sync.dma_start(out=out, in_=result[:])

@@ -72,10 +72,10 @@ def tile_moe_nxt_lin_relu_kernel(tc, xT, w_words, w_scales, b, wp, gate, offs, o
 
         nc.sync.dma_start(out=gate_cols[:], in_=gate[0, :].rearrange("(p i) -> p i", i=PACK))
         load_tokens(0)
-        for q in range(4):
+        for r in range(4):
             nc.sync.dma_start(
-                out=s_raw[32 * q : 32 * q + 4, :, :].bitcast(I32),
-                in_=w_scales[:, 0, 4 * q : 4 * q + 4, :].rearrange("e q n -> q e n").bitcast(I32),
+                out=s_raw[r:P:32, :, :].bitcast(I32),
+                in_=w_scales[:, 0, r:16:4, :].rearrange("e q n -> q e n").bitcast(I32),
             )
         load_tokens(1)
         load_tokens(2)
@@ -130,7 +130,7 @@ def tile_moe_nxt_lin_relu_kernel(tc, xT, w_words, w_scales, b, wp, gate, offs, o
         bias = {(0, 0): bias_own[:, 0, :, 0]}
         for e, a in ((0, 1), (1, 0), (1, 1)):
             own = keep.tile([P, PACK], F32, align_bytes=64, tag="bias%d%d" % (e, a), name="bias%d%d" % (e, a))
-            nc.scalar.copy(out=own[:], in_=bias_own[:, a, :, e])
+            nc.gpsimd.tensor_copy(out=own[:], in_=bias_own[:, a, :, e])
             bias[e, a] = own
 
         slot_codes = []

@@ -58,7 +58,7 @@ def tile_moe_nxt_lin_relu_kernel(tc, xT, w_words, w_scales, b, wp, gate, offs, o
         b_runs = b.rearrange("(a h r) e -> h a (r e)", a=PASSES, r=8)
         wp_rows = wp.rearrange("(a h t i) f -> a i h t f", a=PASSES, t=PACK, i=2)
         x_rows = xT.rearrange("(p j) t -> p j t", j=PACK)
-        chunks = [(0, 256, 96), (256, 256, 96), (512, 128, 48)]
+        chunks = [(0, 256, 160), (256, 256, 128), (512, 128, 64)]
         x_raw = []
         for t0, width, cut in chunks:
             x_raw.append(keep.tile([P, PACK, width], F32, name="x_raw%d" % t0))
@@ -89,7 +89,7 @@ def tile_moe_nxt_lin_relu_kernel(tc, xT, w_words, w_scales, b, wp, gate, offs, o
 
         load_wp(0)
         for i in range(2):
-            nc.sync.dma_start(out=bias_raw[i:P:2, :, 0:14], in_=b_runs[:, :, 2 * i : 2 * i + 14])
+            nc.gpsimd.dma_start(out=bias_raw[i:P:2, :, 0:14], in_=b_runs[:, :, 2 * i : 2 * i + 14])
         load_words(1)
         load_wp(1)
 
@@ -130,7 +130,7 @@ def tile_moe_nxt_lin_relu_kernel(tc, xT, w_words, w_scales, b, wp, gate, offs, o
         bias = {(0, 0): bias_own[:, 0, :, 0]}
         for e, a in ((0, 1), (1, 0), (1, 1)):
             own = keep.tile([P, PACK], F32, align_bytes=64, tag="bias%d%d" % (e, a), name="bias%d%d" % (e, a))
-            nc.gpsimd.tensor_copy(out=own[:], in_=bias_own[:, a, :, e])
+            nc.scalar.copy(out=own[:], in_=bias_own[:, a, :, e])
             bias[e, a] = own
 
         slot_codes = []

@@ -72,10 +72,10 @@ def tile_moe_nxt_lin_relu_kernel(tc, xT, w_words, w_scales, b, wp, gate, offs, o
 
         nc.sync.dma_start(out=gate_cols[:], in_=gate[0, :].rearrange("(p i) -> p i", i=PACK))
         load_tokens(0)
-        for r in range(4):
+        for q in range(4):
             nc.sync.dma_start(
-                out=s_raw[r:P:32, :, :].bitcast(I32),
-                in_=w_scales[:, 0, r:16:4, :].rearrange("e q n -> q e n").bitcast(I32),
+                out=s_raw[32 * q : 32 * q + 4, :, :].bitcast(I32),
+                in_=w_scales[:, 0, 4 * q : 4 * q + 4, :].rearrange("e q n -> q e n").bitcast(I32),
             )
         load_tokens(1)
         load_tokens(2)

@@ -147,7 +147,7 @@ def tile_moe_nxt_lin_relu_kernel(tc, xT, w_words, w_scales, b, wp, gate, offs, o
 
         permute(nc.gpsimd, w_perm[:, 1, :], w_raw[1][:], I32)
         nc.gpsimd.tensor_scalar(
-            out=four(wp_bf[:, 1]), in0=four_in(wp_raw[1][:]), scalar1=1.0, scalar2=0.0, op0=MULT, op1=ADD
+            out=wp_bf[:, 1], in0=wp_raw[1][:].rearrange("p t f -> p f t"), scalar1=1.0, scalar2=0.0, op0=MULT, op1=ADD
         )
 
         def expert(e, a, u0, u1):

@@ -87,10 +87,10 @@ def tile_moe_nxt_lin_relu_kernel(tc, xT, w_words, w_scales, b, wp, gate, offs, o
             for i in range(2):
                 nc.sync.dma_start(out=wp_raw[a][i:P:2, :, :], in_=wp_rows[a, i])
 
-        load_wp(0)
         for i in range(2):
             nc.gpsimd.dma_start(out=bias_raw[i:P:2, :, 0:14], in_=b_runs[:, :, 2 * i : 2 * i + 14])
         load_words(1)
+        load_wp(0)
         load_wp(1)
 
         for i in range(PACK):
@@ -125,7 +125,6 @@ def tile_moe_nxt_lin_relu_kernel(tc, xT, w_words, w_scales, b, wp, gate, offs, o
                 in_=grouped[:].rearrange("p t j -> p (t j)"),
             )
 
-        nc.scalar.copy(out=four(wp_bf[:, 0]), in_=four_in(wp_raw[0][:]))
         bias_own = bias_raw[:].rearrange("p a (t r) -> p a t r", t=PACK)
         bias = {(0, 0): bias_own[:, 0, :, 0]}
         for e, a in ((0, 1), (1, 0), (1, 1)):
@@ -146,9 +145,10 @@ def tile_moe_nxt_lin_relu_kernel(tc, xT, w_words, w_scales, b, wp, gate, offs, o
             slot_scales.append(ss)
 
         permute(nc.gpsimd, w_perm[:, 1, :], w_raw[1][:], I32)
-        nc.gpsimd.tensor_scalar(
-            out=wp_bf[:, 1], in0=wp_raw[1][:].rearrange("p t f -> p f t"), scalar1=1.0, scalar2=0.0, op0=MULT, op1=ADD
-        )
+        for a in range(PASSES):
+            nc.gpsimd.tensor_scalar(
+                out=wp_bf[:, a], in0=wp_raw[a][:].rearrange("p t f -> p f t"), scalar1=1.0, scalar2=0.0, op0=MULT, op1=ADD
+            )
 
         def expert(e, a, u0, u1):
             h = keep.tile([P, PACK, u1 - u0], F32, align_bytes=64, tag="hidden%d%d%d" % (e, a, u0), name="hidden%d%d%d" % (e, a, u0))

@@ -22,6 +22,7 @@ U8 = mybir.dt.uint8
 FP8X4 = mybir.dt.float8_e4m3fn_x4
 FP4X4 = mybir.dt.float4_e2m1fn_x4
 RELU = mybir.ActivationFunctionType.Relu
+COPY = mybir.ActivationFunctionType.Copy
 ADD = mybir.AluOpType.add
 MULT = mybir.AluOpType.mult
 
@@ -30,7 +31,7 @@ def tile_moe_nxt_lin_relu_kernel(tc, xT, w_words, w_scales, b, wp, gate, offs, o
     nc = tc.nc
     with ExitStack() as ctx:
         keep = ctx.enter_context(tc.tile_pool(name="keep", bufs=1))
-        psum1 = ctx.enter_context(tc.psum_pool(name="psum1", bufs=6))
+        psum1 = ctx.enter_context(tc.psum_pool(name="psum1", bufs=7))
         psum2 = ctx.enter_context(tc.psum_pool(name="psum2", bufs=1))
 
         offsets = keep.tile([P, E * C // 16], U16, name="offsets")
@@ -42,13 +43,12 @@ def tile_moe_nxt_lin_relu_kernel(tc, xT, w_words, w_scales, b, wp, gate, offs, o
         scales = keep.tile([P, T], U8, align_bytes=64, name="scales")
         bias_raw = keep.tile([P, PASSES, 16], F32, name="bias_raw")
         gate_cols = keep.tile([P, PACK], F32, name="gate_cols")
-        gates_sb = keep.tile([P, E, SHARE], F32, name="gates_sb")
+        gates_sb = keep.tile([P, E, C], F32, name="gates_sb")
         identity = keep.tile([P, P], F32, name="identity")
         gates = psum2.tile([P, P, PACK], F32, name="gates")
-        accs = psum2.tile([P, E, C], F32, name="accs")
         make_identity(nc, identity[:])
         wp_raw = [keep.tile([P, PACK, M], F32, name="wp_raw%d" % a) for a in range(PASSES)]
-        wp_bf = keep.tile([P, PASSES, M, PACK], BF16, align_bytes=64, name="wp_bf")
+        wp_bf = keep.tile([P, PASSES, M, PACK], BF16, align_bytes=64, tag="wp_bf", name="wp_bf")
         wp_scales = keep.tile([P, PASSES * M], U8, align_bytes=64, name="wp_scales")
         result = keep.tile([P, T], F32, name="result")
 
@@ -96,7 +96,8 @@ def tile_moe_nxt_lin_relu_kernel(tc, xT, w_words, w_scales, b, wp, gate, offs, o
         for i in range(PACK):
             nc.tensor.transpose(gates[:, :, i], gate_cols[:, i : i + 1].to_broadcast([P, P]), identity[:])
         by_slot = gates[:].rearrange("p (e g) i -> p e g i", e=E)
-        nc.scalar.copy(out=gates_sb[:].rearrange("p e (g i) -> p e g i", i=PACK), in_=by_slot[:, :, 0 : SHARE // PACK, :])
+        for e, u0, u1 in ((0, 0, SHARE), (1, 0, SHARE), (1, HALF, HALF + SHARE // 2)):
+            nc.scalar.copy(out=gates_sb[:, e, u0:u1].rearrange("p (g i) -> p g i", i=PACK), in_=by_slot[:, e, u0 // PACK : u1 // PACK, :])
 
         def permute(engine, dst, src, dt):
             line = 4 if dt == I32 else 8
@@ -171,11 +172,11 @@ def tile_moe_nxt_lin_relu_kernel(tc, xT, w_words, w_scales, b, wp, gate, offs, o
         second = expert(0, 0, HALF, C)
         hidden = {(e, a): expert(e, a, 0, C) for e, a in ((0, 1), (1, 0), (1, 1))}
 
-        def on_gpsimd(e, h, g, width):
+        def on_gpsimd(e, h, g, u0, u1):
             nc.gpsimd.tensor_tensor(
                 out=g.rearrange("p (c i) t -> p c t i", i=2),
                 in0=h.rearrange("p t (c i) -> p c t i", i=2),
-                in1=gates_sb[:, e, 0:width].rearrange("p (c i) -> p c i", i=2).unsqueeze(2).to_broadcast([P, width // 2, PACK, 2]),
+                in1=gates_sb[:, e, u0:u1].rearrange("p (c i) -> p c i", i=2).unsqueeze(2).to_broadcast([P, (u1 - u0) // 2, PACK, 2]),
                 op=MULT,
             )
 
@@ -187,9 +188,9 @@ def tile_moe_nxt_lin_relu_kernel(tc, xT, w_words, w_scales, b, wp, gate, offs, o
                 op=MULT,
             )
 
-        def gated(e, a, g):
-            on_gpsimd(e, hidden[e, a][:, :, 0:SHARE], g[:, 0:SHARE, :], SHARE)
-            on_vector(e, hidden[e, a][:, :, SHARE:C], g[:, SHARE:C, :], SHARE, C)
+        def gated(e, a, g, u0, u1, share):
+            on_gpsimd(e, hidden[e, a][:, :, u0 : u0 + share], g[:, 0:share, :], u0, u0 + share)
+            on_vector(e, hidden[e, a][:, :, u0 + share : u1], g[:, share : u1 - u0, :], u0 + share, u1)
 
         def quantised(name, tag, g, width):
             cq = keep.tile([P, width], U32, align_bytes=64, tag=tag, name="c_codes" + name)
@@ -197,45 +198,58 @@ def tile_moe_nxt_lin_relu_kernel(tc, xT, w_words, w_scales, b, wp, gate, offs, o
             nc.vector.quantize_mx(out=cq[:].bitcast(FP8X4), scales=cs[:], in_=g.rearrange("p n t -> p (n t)"))
             return cq, cs
 
-        def project(e, operands):
-            acc = accs[:, e, :]
+        def project(acc, operands):
             for a in range(PASSES):
                 cq, cs = operands[a]
                 nc.tensor.matmul_mx(
                     out=acc,
                     lhsT=wp_codes[:, a * M : (a + 1) * M].bitcast(FP8X4),
                     lhsT_scale=wp_scales[:, a * M : (a + 1) * M],
-                    rhs=cq[:].bitcast(FP8X4),
-                    rhs_scale=cs[:],
+                    rhs=cq.bitcast(FP8X4),
+                    rhs_scale=cs,
                     start=(a == 0),
                     stop=(a == PASSES - 1),
                 )
-            proj = keep.tile([P, C], F32, name="proj%d" % e)
-            nc.scalar.copy(out=proj[:], in_=acc)
-            return proj
 
-        def scatter(e, proj):
-            nc.vector.tensor_copy(result[:].indirect(offsets[:, e * C // 16 : (e + 1) * C // 16]), proj[:])
+        def window(j0, j1):
+            return result[:].indirect(offsets[:, j0 // 16 : j1 // 16])
 
         g00 = keep.tile([P, C, PACK], BF16, align_bytes=64, name="gated00")
-        g01 = keep.tile([P, C, PACK], BF16, align_bytes=64, name="gated01")
-        g10 = keep.tile([P, C, PACK], BF16, align_bytes=64, name="gated10")
-        g11 = keep.tile([P, C, PACK], BF16, align_bytes=64, name="gated11")
         on_vector(0, first[:], g00[:, 0:HALF, :], 0, HALF)
-        on_vector(0, second[:], g00[:, HALF:C, :], HALF, C)
-        wp_codes = keep.tile([P, PASSES * M], U32, align_bytes=64, tag="hidden00128", name="wp_codes")
+        wp_codes = keep.tile([P, PASSES * M], U32, align_bytes=64, tag="hidden000", name="wp_codes")
         nc.vector.quantize_mx(
             out=wp_codes[:].bitcast(FP8X4), scales=wp_scales[:], in_=wp_bf[:].rearrange("p a f t -> p (a f t)")
         )
-        gated(0, 1, g01)
+        on_vector(0, second[:], g00[:, HALF:C, :], HALF, C)
+        g01 = keep.tile([P, C, PACK], BF16, align_bytes=64, tag="wp_bf", name="gated01")
+        gated(0, 1, g01, 0, C, SHARE)
         q00 = quantised("00", "bias01", g00[:], C)
-        gated(1, 0, g10)
-        q01 = quantised("01", "bias10", g01[:], C)
-        gated(1, 1, g11)
+        q01 = quantised("01", "c_codes01", g01[:], C)
+        g10 = keep.tile([P, C, PACK], BF16, align_bytes=64, tag="gated00", name="gated10")
+        gated(1, 0, g10, 0, C, SHARE)
+        g11a = keep.tile([P, HALF, PACK], BF16, align_bytes=64, name="gated11a")
+        gated(1, 1, g11a, 0, HALF, SHARE // 2)
         q10 = quantised("10", "bias11", g10[:], C)
-        q11 = quantised("11", "c_codes11", g11[:], C)
-        p0 = project(0, [q00, q01])
-        p1 = project(1, [q10, q11])
-        scatter(0, p0)
-        scatter(1, p1)
+        q11a = quantised("11a", "c_codes11a", g11a[:], HALF)
+        g11b = keep.tile([P, HALF, PACK], BF16, align_bytes=64, tag="gated00", name="gated11b")
+        gated(1, 1, g11b, HALF, C, SHARE // 2)
+
+        accs = psum1.tile([P, C], F32, tag="bank", name="accs")
+        project(accs[:], [(q00[0][:], q00[1][:]), (q01[0][:], q01[1][:])])
+        p0 = keep.tile([P, C], F32, name="proj0")
+        nc.scalar.copy(out=p0[:], in_=accs[:])
+        nc.scalar.activation(out=window(0, C), in_=p0[:], func=COPY)
+
+        acc_a = psum1.tile([P, HALF], F32, tag="bank", name="acc_a")
+        project(acc_a[:], [(q10[0][:, 0:HALF], q10[1][:, 0:HALF]), (q11a[0][:], q11a[1][:])])
+        p1a = keep.tile([P, HALF], F32, name="proj1a")
+        nc.vector.tensor_copy(out=p1a[:], in_=acc_a[:])
+        nc.scalar.activation(out=window(C, C + HALF), in_=p1a[:], func=COPY)
+
+        q11b = quantised("11b", "c_codes11b", g11b[:], HALF)
+        acc_b = psum1.tile([P, HALF], F32, tag="bank", name="acc_b")
+        project(acc_b[:], [(q10[0][:, HALF:C], q10[1][:, HALF:C]), (q11b[0][:], q11b[1][:])])
+        p1b = keep.tile([P, HALF], F32, name="proj1b")
+        nc.vector.tensor_copy(out=p1b[:], in_=acc_b[:])
+        nc.vector.tensor_copy(out=window(C + HALF, E * C), in_=p1b[:])
         nc.sync.dma_start(out=out, in_=result[:])

from contextlib import ExitStack

import concourse.mybir as mybir
from concourse.masks import make_identity

K, T, E, C, N, M = 512, 640, 2, 256, 1024, 128
P = 128
PACK = 4
PASSES = N // 512
SHARE = 64
HALF = C // 2

FLOPS = 2 * E * C * K * N + 2 * E * C * N * M
BYTES = 4 * K * T + E * K * N // 2 + E * K * N // 32 + 4 * N * E + 4 * N * M + 4 * E * C + 2 * P * (E * C // 16) + 4 * M * T

F32 = mybir.dt.float32
BF16 = mybir.dt.bfloat16
I32 = mybir.dt.int32
U32 = mybir.dt.uint32
U16 = mybir.dt.uint16
U8 = mybir.dt.uint8
FP8X4 = mybir.dt.float8_e4m3fn_x4
FP4X4 = mybir.dt.float4_e2m1fn_x4
RELU = mybir.ActivationFunctionType.Relu
COPY = mybir.ActivationFunctionType.Copy
ADD = mybir.AluOpType.add
MULT = mybir.AluOpType.mult


def tile_moe_nxt_lin_relu_kernel(tc, xT, w_words, w_scales, b, wp, gate, offs, out):
    nc = tc.nc
    with ExitStack() as ctx:
        keep = ctx.enter_context(tc.tile_pool(name="keep", bufs=1))
        psum1 = ctx.enter_context(tc.psum_pool(name="psum1", bufs=7))
        psum2 = ctx.enter_context(tc.psum_pool(name="psum2", bufs=1))

        offsets = keep.tile([P, E * C // 16], U16, name="offsets")
        w_raw = [keep.tile([P, 2 * N], U8, align_bytes=64, tag="w_raw%d" % e, name="w_raw%d" % e) for e in range(E)]
        w_perm = keep.tile([P, E, 2 * N], U8, align_bytes=64, name="w_perm")
        s_raw = keep.tile([P, E, N], U8, align_bytes=64, name="s_raw")
        s_perm = keep.tile([P, E, N], U8, align_bytes=64, name="s_perm")
        codes = keep.tile([P, T], U32, align_bytes=64, name="codes")
        scales = keep.tile([P, T], U8, align_bytes=64, name="scales")
        bias_raw = keep.tile([P, PASSES, 16], F32, name="bias_raw")
        gate_cols = keep.tile([P, PACK], F32, name="gate_cols")
        gates_sb = keep.tile([P, E, C], F32, name="gates_sb")
        identity = keep.tile([P, P], F32, name="identity")
        gates = psum2.tile([P, P, PACK], F32, name="gates")
        make_identity(nc, identity[:])
        wp_raw = [keep.tile([P, PACK, M], F32, name="wp_raw%d" % a) for a in range(PASSES)]
        wp_bf = keep.tile([P, PASSES, M, PACK], BF16, align_bytes=64, tag="wp_bf", name="wp_bf")
        wp_scales = keep.tile([P, PASSES * M], U8, align_bytes=64, name="wp_scales")
        result = keep.tile([P, T], F32, name="result")

        nc.vector.memset(s_raw[:].rearrange("p e n -> p (e n)").bitcast(I32), 0)
        nc.vector.memset(scales[:].bitcast(I32), 0)
        nc.vector.memset(result[:], 0.0)
        b_runs = b.rearrange("(a h r) e -> h a (r e)", a=PASSES, r=8)
        wp_rows = wp.rearrange("(a h t i) f -> a i h t f", a=PASSES, t=PACK, i=2)
        x_rows = xT.rearrange("(p j) t -> p j t", j=PACK)
        chunks = [(0, 256, 160), (256, 256, 128), (512, 128, 64)]
        x_raw = []
        for t0, width, cut in chunks:
            x_raw.append(keep.tile([P, PACK, width], F32, name="x_raw%d" % t0))

        def load_words(e):
            nc.sync.dma_start(out=w_raw[e][:].bitcast(I32), in_=w_words[e, 0].bitcast(I32))

        def load_tokens(n):
            t0, width, cut = chunks[n]
            nc.sync.dma_start(out=x_raw[n][:], in_=x_rows[:, :, t0 : t0 + width])

        nc.sync.dma_start(out=gate_cols[:], in_=gate[0, :].rearrange("(p i) -> p i", i=PACK))
        load_tokens(0)
        for q in range(4):
            nc.sync.dma_start(
                out=s_raw[32 * q : 32 * q + 4, :, :].bitcast(I32),
                in_=w_scales[:, 0, 4 * q : 4 * q + 4, :].rearrange("e q n -> q e n").bitcast(I32),
            )
        load_tokens(1)
        load_tokens(2)
        load_words(0)
        nc.sync.dma_start(offsets[:], offs)


        def load_wp(a):
            for i in range(2):
                nc.sync.dma_start(out=wp_raw[a][i:P:2, :, :], in_=wp_rows[a, i])

        for i in range(2):
            nc.gpsimd.dma_start(out=bias_raw[i:P:2, :, 0:14], in_=b_runs[:, :, 2 * i : 2 * i + 14])
        load_words(1)
        load_wp(0)
        load_wp(1)

        for i in range(PACK):
            nc.tensor.transpose(gates[:, :, i], gate_cols[:, i : i + 1].to_broadcast([P, P]), identity[:])
        by_slot = gates[:].rearrange("p (e g) i -> p e g i", e=E)
        for e, u0, u1 in ((0, 0, SHARE), (1, 0, SHARE), (1, HALF, HALF + SHARE // 2)):
            nc.scalar.copy(out=gates_sb[:, e, u0:u1].rearrange("p (g i) -> p g i", i=PACK), in_=by_slot[:, e, u0 // PACK : u1 // PACK, :])

        def permute(engine, dst, src, dt):
            line = 4 if dt == I32 else 8
            engine.tensor_copy(
                out=dst.bitcast(dt).rearrange("p (a t g h) -> p a g t h", a=PASSES, t=PACK, h=line),
                in_=src.bitcast(dt).rearrange("p (a g h t) -> p a g t h", a=PASSES, t=PACK, h=line),
            )

        permute(nc.vector, w_perm[:, 0, :], w_raw[0][:], I32)
        for e in range(E):
            permute(nc.vector, s_perm[:, e, :], s_raw[:, e, :], U16)

        def four(x):
            return x.rearrange("p (c i) t -> p c t i", i=4)

        def four_in(x):
            return x.rearrange("p t (c i) -> p c t i", i=4)

        for (t0, width, cut), raw in zip(chunks, x_raw):
            grouped = keep.tile([P, width, PACK], BF16, align_bytes=64, name="x_bf%d" % t0)
            nc.scalar.copy(out=four(grouped[:, 0:cut, :]), in_=four_in(raw[:, :, 0:cut]))
            nc.vector.tensor_copy(out=four(grouped[:, cut:width, :]), in_=four_in(raw[:, :, cut:width]))
            nc.vector.quantize_mx(
                out=codes[:, t0 : t0 + width].bitcast(FP8X4),
                scales=scales[:, t0 : t0 + width],
                in_=grouped[:].rearrange("p t j -> p (t j)"),
            )

        bias_own = bias_raw[:].rearrange("p a (t r) -> p a t r", t=PACK)
        bias = {(0, 0): bias_own[:, 0, :, 0]}
        for e, a in ((0, 1), (1, 0), (1, 1)):
            own = keep.tile([P, PACK], F32, align_bytes=64, tag="bias%d%d" % (e, a), name="bias%d%d" % (e, a))
            nc.scalar.copy(out=own[:], in_=bias_own[:, a, :, e])
            bias[e, a] = own

        slot_codes = []
        slot_scales = []
        for e in range(E):
            sc = keep.tile([P, C], U32, align_bytes=64, tag="slot_codes%d" % e, name="slot_codes%d" % e)
            ss = keep.tile([P, C], U8, align_bytes=64, name="slot_scales%d" % e)
            for u0, u1 in ((0, HALF), (HALF, C)) if e == 0 else ((0, C),):
                own = offsets[:, (e * C + u0) // 16 : (e * C + u1) // 16]
                nc.vector.tensor_copy(sc[:, u0:u1], codes[:].indirect(own))
                nc.vector.tensor_copy(ss[:, u0:u1], scales[:].indirect(own))
            slot_codes.append(sc)
            slot_scales.append(ss)

        permute(nc.gpsimd, w_perm[:, 1, :], w_raw[1][:], I32)
        for a in range(PASSES):
            nc.gpsimd.tensor_scalar(
                out=wp_bf[:, a], in0=wp_raw[a][:].rearrange("p t f -> p f t"), scalar1=1.0, scalar2=0.0, op0=MULT, op1=ADD
            )

        def expert(e, a, u0, u1):
            h = keep.tile([P, PACK, u1 - u0], F32, align_bytes=64, tag="hidden%d%d%d" % (e, a, u0), name="hidden%d%d%d" % (e, a, u0))
            for t in range(PACK):
                bank = psum1.tile([P, u1 - u0], F32, name="bank")
                c0 = (a * PACK + t) * P
                nc.tensor.matmul_mx(
                    out=bank[:],
                    lhsT=w_perm[:, e, 2 * c0 : 2 * (c0 + P)].bitcast(FP4X4),
                    lhsT_scale=s_perm[:, e, c0 : c0 + P],
                    rhs=slot_codes[e][:, u0:u1].bitcast(FP8X4),
                    rhs_scale=slot_scales[e][:, u0:u1],
                    start=True,
                    stop=True,
                )
                nc.scalar.activation(out=h[:, t, :], in_=bank[:], func=RELU, bias=bias[e, a][:, t : t + 1])
            return h

        first = expert(0, 0, 0, HALF)
        second = expert(0, 0, HALF, C)
        hidden = {(e, a): expert(e, a, 0, C) for e, a in ((0, 1), (1, 0), (1, 1))}

        def on_gpsimd(e, h, g, u0, u1):
            nc.gpsimd.tensor_tensor(
                out=g.rearrange("p (c i) t -> p c t i", i=2),
                in0=h.rearrange("p t (c i) -> p c t i", i=2),
                in1=gates_sb[:, e, u0:u1].rearrange("p (c i) -> p c i", i=2).unsqueeze(2).to_broadcast([P, (u1 - u0) // 2, PACK, 2]),
                op=MULT,
            )

        def on_vector(e, h, g, u0, u1):
            nc.vector.tensor_tensor(
                out=four(g),
                in0=four_in(h),
                in1=by_slot[:, e, u0 // PACK : u1 // PACK, :].unsqueeze(2).to_broadcast([P, (u1 - u0) // 4, PACK, 4]),
                op=MULT,
            )

        def gated(e, a, g, u0, u1, share):
            on_gpsimd(e, hidden[e, a][:, :, u0 : u0 + share], g[:, 0:share, :], u0, u0 + share)
            on_vector(e, hidden[e, a][:, :, u0 + share : u1], g[:, share : u1 - u0, :], u0 + share, u1)

        def quantised(name, tag, g, width):
            cq = keep.tile([P, width], U32, align_bytes=64, tag=tag, name="c_codes" + name)
            cs = keep.tile([P, width], U8, align_bytes=64, name="c_scales" + name)
            nc.vector.quantize_mx(out=cq[:].bitcast(FP8X4), scales=cs[:], in_=g.rearrange("p n t -> p (n t)"))
            return cq, cs

        def project(acc, operands):
            for a in range(PASSES):
                cq, cs = operands[a]
                nc.tensor.matmul_mx(
                    out=acc,
                    lhsT=wp_codes[:, a * M : (a + 1) * M].bitcast(FP8X4),
                    lhsT_scale=wp_scales[:, a * M : (a + 1) * M],
                    rhs=cq.bitcast(FP8X4),
                    rhs_scale=cs,
                    start=(a == 0),
                    stop=(a == PASSES - 1),
                )

        def window(j0, j1):
            return result[:].indirect(offsets[:, j0 // 16 : j1 // 16])

        g00 = keep.tile([P, C, PACK], BF16, align_bytes=64, name="gated00")
        on_vector(0, first[:], g00[:, 0:HALF, :], 0, HALF)
        wp_codes = keep.tile([P, PASSES * M], U32, align_bytes=64, tag="hidden000", name="wp_codes")
        nc.vector.quantize_mx(
            out=wp_codes[:].bitcast(FP8X4), scales=wp_scales[:], in_=wp_bf[:].rearrange("p a f t -> p (a f t)")
        )
        on_vector(0, second[:], g00[:, HALF:C, :], HALF, C)
        g01 = keep.tile([P, C, PACK], BF16, align_bytes=64, tag="wp_bf", name="gated01")
        gated(0, 1, g01, 0, C, SHARE)
        q00 = quantised("00", "bias01", g00[:], C)
        q01 = quantised("01", "c_codes01", g01[:], C)
        g10 = keep.tile([P, C, PACK], BF16, align_bytes=64, tag="gated00", name="gated10")
        gated(1, 0, g10, 0, C, SHARE)
        g11a = keep.tile([P, HALF, PACK], BF16, align_bytes=64, name="gated11a")
        gated(1, 1, g11a, 0, HALF, SHARE // 2)
        q10 = quantised("10", "bias11", g10[:], C)
        q11a = quantised("11a", "c_codes11a", g11a[:], HALF)
        g11b = keep.tile([P, HALF, PACK], BF16, align_bytes=64, tag="gated00", name="gated11b")
        gated(1, 1, g11b, HALF, C, SHARE // 2)

        accs = psum1.tile([P, C], F32, tag="bank", name="accs")
        project(accs[:], [(q00[0][:], q00[1][:]), (q01[0][:], q01[1][:])])
        p0 = keep.tile([P, C], F32, name="proj0")
        nc.scalar.copy(out=p0[:], in_=accs[:])
        nc.scalar.activation(out=window(0, C), in_=p0[:], func=COPY)

        acc_a = psum1.tile([P, HALF], F32, tag="bank", name="acc_a")
        project(acc_a[:], [(q10[0][:, 0:HALF], q10[1][:, 0:HALF]), (q11a[0][:], q11a[1][:])])
        p1a = keep.tile([P, HALF], F32, name="proj1a")
        nc.vector.tensor_copy(out=p1a[:], in_=acc_a[:])
        nc.scalar.activation(out=window(C, C + HALF), in_=p1a[:], func=COPY)

        q11b = quantised("11b", "c_codes11b", g11b[:], HALF)
        acc_b = psum1.tile([P, HALF], F32, tag="bank", name="acc_b")
        project(acc_b[:], [(q10[0][:, HALF:C], q10[1][:, HALF:C]), (q11b[0][:], q11b[1][:])])
        p1b = keep.tile([P, HALF], F32, name="proj1b")
        nc.vector.tensor_copy(out=p1b[:], in_=acc_b[:])
        nc.vector.tensor_copy(out=window(C + HALF, E * C), in_=p1b[:])
        nc.sync.dma_start(out=out, in_=result[:])
